import numpy as np
import ml_dtypes


def mxq(x, axis, fmt="e4m3"):
    dtype, down = {"e4m3": (ml_dtypes.float8_e4m3fn, 7), "e5m2": (ml_dtypes.float8_e5m2, 14)}[fmt]
    v = np.moveaxis(np.asarray(x, np.float32).astype(ml_dtypes.bfloat16).astype(np.float64), axis, -1)
    blocks = v.reshape(v.shape[:-1] + (-1, 32))
    amax = np.abs(blocks).max(-1, keepdims=True)
    byte = np.maximum(np.where(amax > 0, np.frexp(amax)[1] - 1 + 127, 0) - down, 1)
    scale = np.exp2(byte - 127.0)
    codes = (blocks / scale).astype(np.float32).astype(dtype).astype(np.float64)
    return np.moveaxis((codes * scale).reshape(v.shape), -1, axis)


WIDE = False


def mx_kscale(k):
    if not WIDE:
        return np.ones(k)
    levels = np.array([10, -10, 5, -5, 0])
    if k % 512:
        return np.exp2(np.random.permutation(np.resize(levels, k // 32))).repeat(32)
    a = np.empty((k // 512, 16))
    for p in range(k // 512):
        a[p, :8] = np.random.permutation(np.resize(levels, 8))
        for g in range(8):
            far = levels[np.abs(levels - a[p, g]) >= 10]
            a[p, g + 8] = far[np.random.randint(len(far))]
    return np.exp2(a.ravel()).repeat(32)


def f64(x):
    return np.asarray(x).astype(np.float64)


def striped(idx):
    return np.tile(idx.reshape(-1, 16).T, (8, 1)).astype(np.uint16)


def unstriped(offs):
    return offs[:16].T.reshape(-1).astype(np.int64)


E2M1 = np.array([0.0, 0.5, 1.0, 1.5, 2.0, 3.0, 4.0, 6.0, -0.0, -0.5, -1.0, -1.5, -2.0, -3.0, -4.0, -6.0])


def pack_weight(w, fmt):
    k, n = w.shape
    w = f64(np.asarray(w, np.float32).astype(ml_dtypes.bfloat16)).reshape(k // 32, 32, n)
    amax = np.abs(w).max(1)
    if fmt == "e4m3":
        byte = np.frexp(amax)[1] - 1 + 127 - 7
    else:
        mant, ex = np.frexp(amax / 6.0)
        byte = np.where(mant > 0.5, ex, ex - 1) + 127
    byte = np.clip(np.where(amax > 0, byte, 1), 1, 254)
    scaled = (w * np.exp2(127.0 - byte)[:, None, :]).reshape(k, n).astype(np.float32)
    by_word = np.ascontiguousarray(scaled.reshape(k // 512, 128, 4, n).transpose(0, 1, 3, 2))
    if fmt == "e4m3":
        words = by_word.astype(ml_dtypes.float8_e4m3fn).view(np.uint8)
    else:
        c = by_word.astype(ml_dtypes.float4_e2m1fn).view(np.uint8) & 0xF
        words = (c[..., 0::2] | (c[..., 1::2] << 4)).reshape(k // 512, 128, 2 * n)
    return np.ascontiguousarray(words), np.ascontiguousarray(byte.astype(np.uint8).reshape(k // 512, 16, n))


def unpack_weight(words, scales, fmt):
    g, _, n = scales.shape
    words = np.ascontiguousarray(words).reshape(g, 128, n, -1)
    if fmt == "e4m3":
        vals = words.view(ml_dtypes.float8_e4m3fn).astype(np.float64)
    else:
        nib = np.empty((g, 128, n, 4), np.uint8)
        nib[..., 0::2] = words & 0xF
        nib[..., 1::2] = words >> 4
        vals = E2M1[nib]
    vals = vals * np.repeat(np.exp2(scales.astype(np.float64) - 127.0), 8, axis=1)[..., None]
    return vals.transpose(0, 1, 3, 2).reshape(g * 512, n)


def gelu(v):
    return 0.5 * v * (1.0 + np.tanh(np.sqrt(2.0 / np.pi) * (v + 0.044715 * v**3)))


K, H, T, S, T2, P = 1024, 1536, 2048, 512, 1024, 512


def setup_inputs():
    n = np.random.standard_normal
    s = mx_kscale(K)[:, None]
    u = mx_kscale(H)[:, None]
    d = {}
    d["tab_words"], d["tab_scales"] = pack_weight(n((K, T)) * s, "e4m3")
    d["offs"] = striped(np.random.permutation(T)[:S])
    d["offs2"] = striped(np.random.permutation(T2)[:S])
    d["offs3"] = striped(np.random.permutation(T2)[:P])
    d["wrelief"] = (2.0 * n((K, H)) / K**0.5 / s * u.T).astype(np.float32)
    d["wglare_words"], d["wglare_scales"] = pack_weight(1.5 * n((K, H)) / K**0.5 / s, "e2m1")
    d["page0"] = (n((H, T2)) * u).astype(np.float32)
    d["wgs"] = np.exp(0.3 * n((128, S))).astype(np.float32)
    d["wear"] = (n(H) / H**0.5 / u[:, 0]**2).astype(np.float32)
    d["lim"] = (0.8 * n((T2, P))).astype(np.float32)
    return d


def reference(tab_words, tab_scales, offs, offs2, offs3, wrelief, wglare_words, wglare_scales, page0, wgs, wear, lim):
    v = unpack_weight(tab_words, tab_scales, "e4m3")[:, unstriped(offs)]
    wglare = unpack_weight(wglare_words, wglare_scales, "e2m1")
    relief = mxq(f64(wrelief), 0, "e4m3").T @ v
    glare = wglare.T @ v
    h = relief / (1.0 + np.abs(glare))
    page = f64(page0).copy()
    page[:, unstriped(offs2)] = np.tile(f64(wgs), (H // 128, 1)) * h
    x = np.abs(page[:, unstriped(offs3)]) * f64(wear)[:, None]
    e = mxq(page, 0, "e4m3").T @ mxq(x, 0, "e4m3")
    return np.maximum(e, f64(lim))

@@ -1,0 +1,303 @@
+from contextlib import ExitStack
+
+import concourse.mybir as mybir
+
+K, H, T, S, T2, NX = 1024, 1536, 2048, 512, 1024, 512
+FLOPS = 2 * (2 * K * H * S + H * T2 * NX)
+
+F32 = mybir.dt.float32
+BF16 = mybir.dt.bfloat16
+I32 = mybir.dt.int32
+U32 = mybir.dt.uint32
+U16 = mybir.dt.uint16
+U8 = mybir.dt.uint8
+FP8X4 = mybir.dt.float8_e4m3fn_x4
+FP4X4 = mybir.dt.float4_e2m1fn_x4
+ACT = mybir.ActivationFunctionType
+ALU = mybir.AluOpType
+
+P = 128
+PACK = 4
+KP = P * PACK
+NA = K // KP
+NB = H // KP
+NT = NB * PACK
+NM = T2 // P
+
+
+def tile_list_die_wear_match_kernel(
+    tc, tab_words, tab_scales, offs, offs2, offs3, wrelief, wglare_words, wglare_scales, page0, wgs, wear, lim, out
+):
+    nc = tc.nc
+    with ExitStack() as ctx:
+        keep = ctx.enter_context(tc.tile_pool(name="keep", bufs=1))
+        big = ctx.enter_context(tc.tile_pool(name="big", bufs=2))
+        wrawp = ctx.enter_context(tc.tile_pool(name="wraw", bufs=3))
+        two = ctx.enter_context(tc.tile_pool(name="two", bufs=2))
+        three = ctx.enter_context(tc.tile_pool(name="three", bufs=3))
+        damp = ctx.enter_context(tc.tile_pool(name="damp", bufs=5))
+        pagep = ctx.enter_context(tc.tile_pool(name="pages", bufs=6))
+        psum = ctx.enter_context(tc.psum_pool(name="psum", bufs=8))
+
+        o1 = keep.tile([P, S // 16], U16, name="o1")
+        o2 = keep.tile([P, S // 16], U16, name="o2")
+        o3 = keep.tile([P, NX // 16], U16, name="o3")
+        tsc = keep.tile([P, NA, T], U8, name="tsc", align_bytes=64)
+        gsc_raw = keep.tile([P, NA, H], U8, name="gsc_raw", align_bytes=64)
+        nc.vector.memset(tsc[:].bitcast(I32), 0)
+        nc.vector.memset(gsc_raw[:].bitcast(I32), 0)
+
+        nc.sync.dma_start(o1[:], offs)
+        tw = []
+        for a in range(NA):
+            w = big.tile([P, T], I32, name="tw", tag="big", align_bytes=64)
+            nc.sync.dma_start(out=w[:], in_=tab_words[a].rearrange("p t i -> p (t i)").bitcast(I32))
+            tw.append(w)
+            if a == 0:
+                for q in range(4):
+                    nc.sync.dma_start(
+                        out=tsc[32 * q : 32 * q + 4].bitcast(I32),
+                        in_=tab_scales[:, 4 * q : 4 * q + 4, :].rearrange("a r t -> r a t").bitcast(I32),
+                    )
+                gw_raw = keep.tile([P, NA, 2 * H], U8, name="gw_raw", align_bytes=64)
+                nc.sync.dma_start(out=gw_raw[:].bitcast(I32), in_=wglare_words.rearrange("a p c -> p a c").bitcast(I32))
+        for q in range(4):
+            nc.sync.dma_start(
+                out=gsc_raw[32 * q : 32 * q + 4].bitcast(I32),
+                in_=wglare_scales[:, 4 * q : 4 * q + 4, :].rearrange("a r c -> r a c").bitcast(I32),
+            )
+
+        wraw = {}
+
+        def load_w(b, a):
+            w = wrawp.tile([P, PACK, KP], F32, name="wraw")
+            nc.sync.dma_start(
+                out=w[:], in_=wrelief[KP * a : KP * (a + 1), KP * b : KP * (b + 1)].rearrange("(p j) c -> p j c", j=PACK)
+            )
+            wraw[b, a] = w
+
+        pages = {}
+
+        def load_page(i):
+            b, t = divmod(i, PACK)
+            pg = pagep.tile([P, T2], F32, name="pg")
+            nc.sync.dma_start(out=pg[:], in_=page0[KP * b : KP * (b + 1), :].rearrange("(p t) m -> p t m", t=PACK)[:, t, :])
+            pages[i] = pg
+
+        load_w(0, 0)
+        load_w(0, 1)
+        wg0 = keep.tile([P, S], F32, name="wg0")
+        wg1 = keep.tile([P, PACK - 1, S], F32, name="wg1")
+        wgv = wgs.rearrange("(p t) j -> p t j", t=PACK)
+        for q in range(4):
+            nc.sync.dma_start(out=wg0[32 * q : 32 * q + 32], in_=wgv[:, 0, :])
+        nc.sync.dma_start(o2[:], offs2)
+        load_page(0)
+        for q in range(4):
+            nc.sync.dma_start(out=wg1[32 * q : 32 * q + 32], in_=wgv[:, 1:, :])
+        wg = [wg0[:]] + [wg1[:, t, :] for t in range(PACK - 1)]
+        nc.sync.dma_start(o3[:], offs3)
+        wr = keep.tile([P, NB, PACK], F32, name="wr")
+        nc.sync.dma_start(out=wr[:], in_=wear.rearrange("(b p t) -> p b t", p=P, t=PACK))
+        load_page(1)
+        load_page(2)
+
+        vw, vs = [], []
+        for a in range(NA):
+            w = keep.tile([P, S], U32, name=f"vw{a}", align_bytes=64)
+            nc.vector.tensor_copy(w[:], tw[a][:].bitcast(U32).indirect(o1[:]))
+            vw.append(w)
+        for a in range(NA):
+            s = keep.tile([P, S], U8, name=f"vs{a}", align_bytes=64)
+            nc.vector.tensor_copy(s[:], tsc[:, a, :].indirect(o1[:]))
+            vs.append(s)
+
+        gw, gsc = [], []
+        for b in range(NB):
+            w = keep.tile([P, NA, PACK, 2 * P], U8, name=f"gw{b}", align_bytes=64)
+            sc = keep.tile([P, NA, PACK, P], U8, name=f"gsc{b}", align_bytes=64)
+            nc.scalar.copy(
+                out=w[:].bitcast(U16),
+                in_=gw_raw[:].bitcast(U16)[:, :, KP * b : KP * (b + 1)].rearrange("p a (q t) -> p a t q", t=PACK),
+            )
+            nc.vector.tensor_copy(
+                out=sc[:], in_=gsc_raw[:, :, KP * b : KP * (b + 1)].rearrange("p a (q t) -> p a t q", t=PACK)
+            )
+            gw.append(w)
+            gsc.append(sc)
+
+        wcodes, wscales = {}, {}
+
+        def prep_w(b, a, copy):
+            if a == 0:
+                wcodes[b] = two.tile([P, NA, KP], U32, name="wcodes", align_bytes=64)
+                wscales[b] = two.tile([P, NA, KP], U8, name="wscales", align_bytes=64)
+            wi = two.tile([P, PACK, P, PACK], BF16, name="wi", align_bytes=64)
+            copy(
+                out=wi[:].rearrange("p t m j -> p m j t"),
+                in_=wraw[b, a][:].rearrange("p j (m t) -> p m j t", t=PACK),
+            )
+            nc.vector.quantize_mx(
+                out=wcodes[b][:, a, :].bitcast(FP8X4),
+                scales=wscales[b][:, a, :],
+                in_=wi[:].rearrange("p t m j -> p (t m j)"),
+            )
+
+        damps, nums, gath = {}, {}, {}
+
+        def glare(i):
+            b, t = divmod(i, PACK)
+            bank = psum.tile([P, S], F32, name="bank", tag="bank")
+            for a in range(NA):
+                nc.tensor.matmul_mx(
+                    out=bank[:],
+                    lhsT=gw[b][:, a, t, :].bitcast(FP4X4),
+                    lhsT_scale=gsc[b][:, a, t, :],
+                    rhs=vw[a][:].bitcast(FP8X4),
+                    rhs_scale=vs[a][:],
+                    start=(a == 0),
+                    stop=(a == NA - 1),
+                )
+            mag = two.tile([P, S], F32, name="mag")
+            nc.scalar.activation(out=mag[:], in_=bank[:], func=ACT.Abs)
+            root = two.tile([P, S], F32, name="root")
+            nc.scalar.activation(out=root[:], in_=mag[:], func=ACT.Abs_reciprocal_sqrt, bias=1.0)
+            d = damp.tile([P, S], F32, name="d")
+            nc.scalar.activation(out=d[:], in_=root[:], func=ACT.Square)
+            damps[i] = d
+
+        def relief(i):
+            b, t = divmod(i, PACK)
+            bank = psum.tile([P, S], F32, name="bank", tag="bank")
+            for a in range(NA):
+                nc.tensor.matmul_mx(
+                    out=bank[:],
+                    lhsT=wcodes[b][:, a, P * t : P * (t + 1)].bitcast(FP8X4),
+                    lhsT_scale=wscales[b][:, a, P * t : P * (t + 1)],
+                    rhs=vw[a][:].bitcast(FP8X4),
+                    rhs_scale=vs[a][:],
+                    start=(a == 0),
+                    stop=(a == NA - 1),
+                )
+            n = three.tile([P, S], F32, name="num")
+            nc.vector.tensor_tensor(out=n[:], in0=bank[:], in1=wg[t], op=ALU.mult)
+            nums[i] = n
+
+        def put(i):
+            nc.vector.tensor_tensor(out=pages[i][:].indirect(o2[:]), in0=nums[i][:], in1=damps[i][:], op=ALU.mult)
+
+        def fetch(i):
+            g = two.tile([P, NX], F32, name="g") if i < NT - 2 else keep.tile([P, NX], F32, name=f"g{i}")
+            nc.vector.tensor_copy(g[:], pages[i][:].indirect(o3[:]))
+            gath[i] = g
+
+        pplanes, xplanes = {}, {}
+
+        def round_page(i):
+            b, t = divmod(i, PACK)
+            if t == 0:
+                pplanes[b] = two.tile([P, PACK, T2], BF16, name="pplanes")
+            nc.gpsimd.tensor_scalar(
+                out=pplanes[b][:, t, :], in0=pages[i][:], scalar1=1.0, scalar2=0.0, op0=ALU.mult, op1=ALU.add
+            )
+
+        def round_rows(i):
+            b, t = divmod(i, PACK)
+            if t == 0:
+                xplanes[b] = two.tile([P, PACK, NX], BF16, name="xplanes")
+            ga = two.tile([P, NX], F32, name="ga")
+            nc.scalar.activation(out=ga[:], in_=gath[i][:], func=ACT.Abs)
+            nc.scalar.activation(out=xplanes[b][:, t, :], in_=ga[:], func=ACT.Copy, scale=wr[:, b, t : t + 1])
+
+        pcodes = [[keep.tile([P, KP], U32, name=f"pc{b}{hh}", align_bytes=64) for hh in range(2)] for b in range(NB)]
+        pscales = [[keep.tile([P, KP], U8, name=f"ps{b}{hh}", align_bytes=64) for hh in range(2)] for b in range(NB)]
+        xcodes = [keep.tile([P, NX], U32, name=f"xc{b}", align_bytes=64) for b in range(NB)]
+        xscales = [keep.tile([P, NX], U8, name=f"xs{b}", align_bytes=64) for b in range(NB)]
+
+        def weave(dst, planes, c0, c1, d0, copy):
+            copy(
+                out=dst[:, d0 : d0 + c1 - c0, :].rearrange("p (c i) t -> p c t i", i=4),
+                in_=planes[:, :, c0:c1].rearrange("p t (c i) -> p c t i", i=4),
+            )
+
+        def quant(src, codes, scales):
+            nc.vector.quantize_mx(out=codes.bitcast(FP8X4), scales=scales, in_=src[:].rearrange("p c t -> p (c t)"))
+
+        def page_half(b, hh, copy):
+            wv = three.tile([P, KP, PACK], BF16, name="wv", align_bytes=64)
+            weave(wv, pplanes[b], KP * hh, KP * (hh + 1), 0, copy)
+            quant(wv, pcodes[b][hh][:], pscales[b][hh][:])
+
+        def x_group(b):
+            wv = three.tile([P, KP, PACK], BF16, name="wv", align_bytes=64)
+            if b < NB - 1:
+                weave(wv, xplanes[b], 0, NX, 0, nc.scalar.copy)
+            else:
+                weave(wv, xplanes[b], 0, 320, 0, nc.vector.tensor_copy)
+                weave(wv, xplanes[b], 320, NX, 320, nc.scalar.copy)
+            quant(wv, xcodes[b][:], xscales[b][:])
+
+        glare(0)
+        prep_w(0, 0, nc.vector.tensor_copy)
+        prep_w(0, 1, nc.vector.tensor_copy)
+        relief(0)
+        lims = []
+        for i in range(NT):
+            b, t = divmod(i, PACK)
+            if i + 3 < NT:
+                load_page(i + 3)
+            if i < 4:
+                load_w(1 + i // 2, i % 2)
+            if i == 2 * PACK:
+                for hh in range(2):
+                    lm = big.tile([P, NM // 2, NX], F32, name="lm", tag="big", align_bytes=64)
+                    nc.sync.dma_start(out=lm[:], in_=lim[KP * hh : KP * (hh + 1), :].rearrange("(c p) j -> p c j", p=P))
+                    lims.append(lm)
+            if i + 1 < NT:
+                glare(i + 1)
+            put(i)
+            round_page(i)
+            if 1 <= i:
+                fetch(i - 1)
+            if i + 1 < NT:
+                relief(i + 1)
+            if 1 <= i <= 4:
+                prep_w(1 + (i - 1) // 2, (i - 1) % 2, nc.scalar.copy)
+            if i >= 2:
+                round_rows(i - 2)
+            if i in (5, 6):
+                page_half(0, i - 5, nc.scalar.copy)
+            if i in (8, 9):
+                page_half(1, i - 8, nc.scalar.copy)
+            if i in (7, 9):
+                x_group((i - 7) // 2)
+        def score_pass(bank, m, b):
+            nc.tensor.matmul_mx(
+                out=bank[:],
+                lhsT=pcodes[b][m // 4][:, P * (m % 4) : P * (m % 4 + 1)].bitcast(FP8X4),
+                lhsT_scale=pscales[b][m // 4][:, P * (m % 4) : P * (m % 4 + 1)],
+                rhs=xcodes[b][:].bitcast(FP8X4),
+                rhs_scale=xscales[b][:],
+                start=(b == 0),
+                stop=(b == NB - 1),
+            )
+
+        banks = []
+        for m in range(NM):
+            bank = psum.tile([P, NX], F32, name="bank", tag="bank")
+            score_pass(bank, m, 0)
+            banks.append(bank)
+        for m in range(NM):
+            score_pass(banks[m], m, 1)
+        round_rows(NT - 2)
+        fetch(NT - 1)
+        round_rows(NT - 1)
+        page_half(NB - 1, 0, nc.vector.tensor_copy)
+        x_group(NB - 1)
+        page_half(NB - 1, 1, nc.scalar.copy)
+
+        for m in range(NM):
+            score_pass(banks[m], m, NB - 1)
+            res = three.tile([P, NX], F32, name="res")
+            nc.vector.tensor_tensor(out=res[:], in0=banks[m][:], in1=lims[m // 4][:, m % 4, :], op=ALU.max)
+            nc.sync.dma_start(out=out[P * m : P * (m + 1), :], in_=res[:])

@@ -35,8 +35,8 @@ def tile_list_die_wear_match_kernel(
         wrawp = ctx.enter_context(tc.tile_pool(name="wraw", bufs=3))
         two = ctx.enter_context(tc.tile_pool(name="two", bufs=2))
         three = ctx.enter_context(tc.tile_pool(name="three", bufs=3))
-        damp = ctx.enter_context(tc.tile_pool(name="damp", bufs=5))
-        pagep = ctx.enter_context(tc.tile_pool(name="pages", bufs=6))
+        damp = ctx.enter_context(tc.tile_pool(name="damp", bufs=3))
+        pagep = ctx.enter_context(tc.tile_pool(name="pages", bufs=5))
         psum = ctx.enter_context(tc.psum_pool(name="psum", bufs=8))
 
         o1 = keep.tile([P, S // 16], U16, name="o1")
@@ -85,7 +85,13 @@ def tile_list_die_wear_match_kernel(
             pages[i] = pg
 
         load_w(0, 0)
-        load_w(0, 1)
+        whalf = []
+        for hh in range(2):
+            w = two.tile([P, PACK, KP // 2], F32, name="whalf")
+            nc.sync.dma_start(
+                out=w[:], in_=wrelief[KP : 2 * KP, 256 * hh : 256 * (hh + 1)].rearrange("(p j) c -> p j c", j=PACK)
+            )
+            whalf.append(w)
         wg0 = keep.tile([P, S], F32, name="wg0")
         wg1 = keep.tile([P, PACK - 1, S], F32, name="wg1")
         wgv = wgs.rearrange("(p t) j -> p t j", t=PACK)
@@ -112,8 +118,9 @@ def tile_list_die_wear_match_kernel(
             nc.vector.tensor_copy(s[:], tsc[:, a, :].indirect(o1[:]))
             vs.append(s)
 
-        gw, gsc = [], []
-        for b in range(NB):
+        gw, gsc = {}, {}
+
+        def deal_glare(b):
             w = keep.tile([P, NA, PACK, 2 * P], U8, name=f"gw{b}", align_bytes=64)
             sc = keep.tile([P, NA, PACK, P], U8, name=f"gsc{b}", align_bytes=64)
             nc.scalar.copy(
@@ -123,8 +130,8 @@ def tile_list_die_wear_match_kernel(
             nc.vector.tensor_copy(
                 out=sc[:], in_=gsc_raw[:, :, KP * b : KP * (b + 1)].rearrange("p a (q t) -> p a t q", t=PACK)
             )
-            gw.append(w)
-            gsc.append(sc)
+            gw[b] = w
+            gsc[b] = sc
 
         wcodes, wscales = {}, {}
 
@@ -158,9 +165,9 @@ def tile_list_die_wear_match_kernel(
                     start=(a == 0),
                     stop=(a == NA - 1),
                 )
-            mag = two.tile([P, S], F32, name="mag")
+            mag = keep.tile([P, S], F32, name="mag", tag=f"m{i % 2}")
             nc.scalar.activation(out=mag[:], in_=bank[:], func=ACT.Abs)
-            root = two.tile([P, S], F32, name="root")
+            root = keep.tile([P, S], F32, name="root", tag=f"r{i % 4}")
             nc.scalar.activation(out=root[:], in_=mag[:], func=ACT.Abs_reciprocal_sqrt, bias=1.0)
             d = damp.tile([P, S], F32, name="d")
             nc.scalar.activation(out=d[:], in_=root[:], func=ACT.Square)
@@ -179,7 +186,7 @@ def tile_list_die_wear_match_kernel(
                     start=(a == 0),
                     stop=(a == NA - 1),
                 )
-            n = three.tile([P, S], F32, name="num")
+            n = keep.tile([P, S], F32, name="num", tag=f"r{(i - 1) % 4}")
             nc.vector.tensor_tensor(out=n[:], in0=bank[:], in1=wg[t], op=ALU.mult)
             nums[i] = n
 
@@ -187,7 +194,7 @@ def tile_list_die_wear_match_kernel(
             nc.vector.tensor_tensor(out=pages[i][:].indirect(o2[:]), in0=nums[i][:], in1=damps[i][:], op=ALU.mult)
 
         def fetch(i):
-            g = two.tile([P, NX], F32, name="g") if i < NT - 2 else keep.tile([P, NX], F32, name=f"g{i}")
+            g = keep.tile([P, NX], F32, name="g", tag=f"g{i % 2}")
             nc.vector.tensor_copy(g[:], pages[i][:].indirect(o3[:]))
             gath[i] = g
 
@@ -205,7 +212,7 @@ def tile_list_die_wear_match_kernel(
             b, t = divmod(i, PACK)
             if t == 0:
                 xplanes[b] = two.tile([P, PACK, NX], BF16, name="xplanes")
-            ga = two.tile([P, NX], F32, name="ga")
+            ga = keep.tile([P, NX], F32, name="ga", tag=f"m{(i + 1) % 2}")
             nc.scalar.activation(out=ga[:], in_=gath[i][:], func=ACT.Abs)
             nc.scalar.activation(out=xplanes[b][:, t, :], in_=ga[:], func=ACT.Copy, scale=wr[:, b, t : t + 1])
 
@@ -230,17 +237,27 @@ def tile_list_die_wear_match_kernel(
 
         def x_group(b):
             wv = three.tile([P, KP, PACK], BF16, name="wv", align_bytes=64)
-            if b < NB - 1:
-                weave(wv, xplanes[b], 0, NX, 0, nc.scalar.copy)
-            else:
-                weave(wv, xplanes[b], 0, 320, 0, nc.vector.tensor_copy)
-                weave(wv, xplanes[b], 320, NX, 320, nc.scalar.copy)
+            weave(wv, xplanes[b], 0, NX, 0, nc.scalar.copy)
             quant(wv, xcodes[b][:], xscales[b][:])
 
+        deal_glare(0)
         glare(0)
         prep_w(0, 0, nc.vector.tensor_copy)
-        prep_w(0, 1, nc.vector.tensor_copy)
+        wi = two.tile([P, PACK, P, PACK], BF16, name="wi", align_bytes=64)
+        for hh in range(2):
+            nc.vector.tensor_copy(
+                out=wi[:, :, 64 * hh : 64 * (hh + 1), :].rearrange("p t m j -> p m j t"),
+                in_=whalf[hh][:].rearrange("p j (m t) -> p m j t", t=PACK),
+            )
+        for t0, t1 in ((0, 1), (1, PACK)):
+            nc.vector.quantize_mx(
+                out=wcodes[0][:, 1, P * t0 : P * t1].bitcast(FP8X4),
+                scales=wscales[0][:, 1, P * t0 : P * t1],
+                in_=wi[:, t0:t1].rearrange("p t m j -> p (t m j)"),
+            )
         relief(0)
+        deal_glare(1)
+        deal_glare(2)
         lims = []
         for i in range(NT):
             b, t = divmod(i, PACK)
@@ -253,24 +270,24 @@ def tile_list_die_wear_match_kernel(
                     lm = big.tile([P, NM // 2, NX], F32, name="lm", tag="big", align_bytes=64)
                     nc.sync.dma_start(out=lm[:], in_=lim[KP * hh : KP * (hh + 1), :].rearrange("(c p) j -> p c j", p=P))
                     lims.append(lm)
-            if i + 1 < NT:
-                glare(i + 1)
+            if i >= 1:
+                glare(i)
             put(i)
             round_page(i)
-            if 1 <= i:
-                fetch(i - 1)
             if i + 1 < NT:
                 relief(i + 1)
-            if 1 <= i <= 4:
-                prep_w(1 + (i - 1) // 2, (i - 1) % 2, nc.scalar.copy)
             if i >= 2:
                 round_rows(i - 2)
+            if i < NT - 1:
+                fetch(i)
+            if 1 <= i <= 4:
+                prep_w(1 + (i - 1) // 2, (i - 1) % 2, nc.scalar.copy)
             if i in (5, 6):
                 page_half(0, i - 5, nc.scalar.copy)
             if i in (8, 9):
                 page_half(1, i - 8, nc.scalar.copy)
-            if i in (7, 9):
-                x_group((i - 7) // 2)
+            if i in (7, 10):
+                x_group((i - 7) // 3)
         def score_pass(bank, m, b):
             nc.tensor.matmul_mx(
                 out=bank[:],
@@ -290,14 +307,40 @@ def tile_list_die_wear_match_kernel(
         for m in range(NM):
             score_pass(banks[m], m, 1)
         round_rows(NT - 2)
-        fetch(NT - 1)
-        round_rows(NT - 1)
-        page_half(NB - 1, 0, nc.vector.tensor_copy)
-        x_group(NB - 1)
-        page_half(NB - 1, 1, nc.scalar.copy)
+        last = NT - 1
+        Q = 256
+        g = keep.tile([P, NX], F32, name="g", tag=f"g{last % 2}")
+        ga = keep.tile([P, NX], F32, name="ga", tag=f"m{(last + 1) % 2}")
+        for hh in range(2):
+            cols = slice(Q * hh, Q * (hh + 1))
+            nc.vector.tensor_copy(g[:, cols], pages[last][:].indirect(o3[:, 16 * hh : 16 * (hh + 1)]))
+            nc.scalar.activation(out=ga[:, cols], in_=g[:, cols], func=ACT.Abs)
+            nc.scalar.activation(
+                out=xplanes[NB - 1][:, PACK - 1, cols], in_=ga[:, cols], func=ACT.Copy, scale=wr[:, NB - 1, PACK - 1 : PACK]
+            )
+
+        def quarter(planes, c0, copy):
+            wq = keep.tile([P, Q, PACK], BF16, name="wq", tag=f"wq{len(quarters)}", align_bytes=64)
+            weave(wq, planes, c0, c0 + Q, 0, copy)
+            quarters.append(wq)
+            return wq
+
+        def quant_page_quarter(k, wq):
+            cols = slice(Q * (k % 2), Q * (k % 2 + 1))
+            quant(wq, pcodes[NB - 1][k // 2][:, cols], pscales[NB - 1][k // 2][:, cols])
+
+        quarters = []
+        p0 = quarter(pplanes[NB - 1], 0, nc.vector.tensor_copy)
+        xa = quarter(xplanes[NB - 1], 0, nc.vector.tensor_copy)
+        xb = quarter(xplanes[NB - 1], Q, nc.scalar.copy)
+        quant_page_quarter(0, p0)
+        quant(xa, xcodes[NB - 1][:, 0:Q], xscales[NB - 1][:, 0:Q])
+        quant(xb, xcodes[NB - 1][:, Q:], xscales[NB - 1][:, Q:])
 
         for m in range(NM):
+            if m % 2 == 0 and m + 2 < NM:
+                quant_page_quarter(m // 2 + 1, quarter(pplanes[NB - 1], Q * (m // 2 + 1), nc.scalar.copy))
             score_pass(banks[m], m, NB - 1)
-            res = three.tile([P, NX], F32, name="res")
-            nc.vector.tensor_tensor(out=res[:], in0=banks[m][:], in1=lims[m // 4][:, m % 4, :], op=ALU.max)
-            nc.sync.dma_start(out=out[P * m : P * (m + 1), :], in_=res[:])
+            res = lims[m // 4][:, m % 4, :]
+            nc.vector.tensor_tensor(out=res, in0=banks[m][:], in1=res, op=ALU.max)
+            nc.sync.dma_start(out=out[P * m : P * (m + 1), :], in_=res)

@@ -18,11 +18,20 @@ ALU = mybir.AluOpType
 
 P = 128
 PACK = 4
-KP = P * PACK
-NA = K // KP
-NB = H // KP
-NT = NB * PACK
-NM = T2 // P
+PASS = P * PACK
+K_PASSES = K // PASS
+GROUPS = H // PASS
+SETS = GROUPS * PACK
+OUT_TILES = T2 // P
+QUADRANTS = 4
+SCALE_ROWS = 4
+LIST_ROWS = 16
+RUN = 4
+QUARTER = T2 // 4
+X_ON_VECTOR = 384
+PAGES_AHEAD = 3
+ROUND_LAG = 2
+EARLY_SETS = 3
 
 
 def tile_list_die_wear_match_kernel(
@@ -32,315 +41,329 @@ def tile_list_die_wear_match_kernel(
     with ExitStack() as ctx:
         keep = ctx.enter_context(tc.tile_pool(name="keep", bufs=1))
         big = ctx.enter_context(tc.tile_pool(name="big", bufs=2))
-        wrawp = ctx.enter_context(tc.tile_pool(name="wraw", bufs=3))
+        wraw_pool = ctx.enter_context(tc.tile_pool(name="wraw", bufs=3))
         two = ctx.enter_context(tc.tile_pool(name="two", bufs=2))
         three = ctx.enter_context(tc.tile_pool(name="three", bufs=3))
-        damp = ctx.enter_context(tc.tile_pool(name="damp", bufs=3))
-        pagep = ctx.enter_context(tc.tile_pool(name="pages", bufs=5))
-        psum = ctx.enter_context(tc.psum_pool(name="psum", bufs=8))
+        damp_pool = ctx.enter_context(tc.tile_pool(name="damp", bufs=3))
+        page_pool = ctx.enter_context(tc.tile_pool(name="pages", bufs=PAGES_AHEAD + ROUND_LAG + 1))
+        psum = ctx.enter_context(tc.psum_pool(name="psum", bufs=1))
 
-        o1 = keep.tile([P, S // 16], U16, name="o1")
-        o2 = keep.tile([P, S // 16], U16, name="o2")
-        o3 = keep.tile([P, NX // 16], U16, name="o3")
-        tsc = keep.tile([P, NA, T], U8, name="tsc", align_bytes=64)
-        gsc_raw = keep.tile([P, NA, H], U8, name="gsc_raw", align_bytes=64)
-        nc.vector.memset(tsc[:].bitcast(I32), 0)
-        nc.vector.memset(gsc_raw[:].bitcast(I32), 0)
+        pick = keep.tile([P, S // LIST_ROWS], U16, name="pick")
+        slot = keep.tile([P, S // LIST_ROWS], U16, name="slot")
+        ref = keep.tile([P, NX // LIST_ROWS], U16, name="ref")
+        tab_sc = keep.tile([P, K_PASSES, T], U8, name="tab_sc", align_bytes=64)
+        glare_sc_raw = keep.tile([P, K_PASSES, H], U8, name="glare_sc_raw", align_bytes=64)
+        nc.vector.memset(glare_sc_raw[:].bitcast(I32), 0)
+        nc.vector.memset(tab_sc[:].bitcast(I32), 0)
 
-        nc.sync.dma_start(o1[:], offs)
-        tw = []
-        for a in range(NA):
-            w = big.tile([P, T], I32, name="tw", tag="big", align_bytes=64)
-            nc.sync.dma_start(out=w[:], in_=tab_words[a].rearrange("p t i -> p (t i)").bitcast(I32))
-            tw.append(w)
-            if a == 0:
-                for q in range(4):
-                    nc.sync.dma_start(
-                        out=tsc[32 * q : 32 * q + 4].bitcast(I32),
-                        in_=tab_scales[:, 4 * q : 4 * q + 4, :].rearrange("a r t -> r a t").bitcast(I32),
-                    )
-                gw_raw = keep.tile([P, NA, 2 * H], U8, name="gw_raw", align_bytes=64)
-                nc.sync.dma_start(out=gw_raw[:].bitcast(I32), in_=wglare_words.rearrange("a p c -> p a c").bitcast(I32))
-        for q in range(4):
+        def load_scale_rows(dst, scales):
+            for q in range(QUADRANTS):
+                nc.sync.dma_start(
+                    out=dst[32 * q : 32 * q + SCALE_ROWS].bitcast(I32),
+                    in_=scales[:, SCALE_ROWS * q : SCALE_ROWS * (q + 1), :].rearrange("a r c -> r a c").bitcast(I32),
+                )
+
+        def load_table(a):
+            words = big.tile([P, T], I32, name="tab_w", tag="big", align_bytes=64)
+            nc.sync.dma_start(out=words[:], in_=tab_words[a].rearrange("p t i -> p (t i)").bitcast(I32))
+            return words
+
+        def load_glare_words(name, c0, c1):
+            raw = keep.tile([P, K_PASSES, 2 * (c1 - c0)], U8, name=name, align_bytes=64)
             nc.sync.dma_start(
-                out=gsc_raw[32 * q : 32 * q + 4].bitcast(I32),
-                in_=wglare_scales[:, 4 * q : 4 * q + 4, :].rearrange("a r c -> r a c").bitcast(I32),
+                out=raw[:].bitcast(I32), in_=wglare_words.rearrange("a p c -> p a c")[:, :, 2 * c0 : 2 * c1].bitcast(I32)
             )
+            return raw[:].bitcast(U16)
 
-        wraw = {}
+        def wrelief_rows(a, c0, c1):
+            return wrelief[PASS * a : PASS * (a + 1), c0:c1].rearrange("(p j) c -> p j c", j=PACK)
 
-        def load_w(b, a):
-            w = wrawp.tile([P, PACK, KP], F32, name="wraw")
-            nc.sync.dma_start(
-                out=w[:], in_=wrelief[KP * a : KP * (a + 1), KP * b : KP * (b + 1)].rearrange("(p j) c -> p j c", j=PACK)
-            )
-            wraw[b, a] = w
+        wraw, pages = {}, {}
 
-        pages = {}
+        def load_wrelief(b, a):
+            wraw[b, a] = wraw_pool.tile([P, PACK, PASS], F32, name="wraw")
+            nc.sync.dma_start(out=wraw[b, a][:], in_=wrelief_rows(a, PASS * b, PASS * (b + 1)))
 
         def load_page(i):
             b, t = divmod(i, PACK)
-            pg = pagep.tile([P, T2], F32, name="pg")
-            nc.sync.dma_start(out=pg[:], in_=page0[KP * b : KP * (b + 1), :].rearrange("(p t) m -> p t m", t=PACK)[:, t, :])
-            pages[i] = pg
+            pages[i] = page_pool.tile([P, T2], F32, name="page")
+            rows = page0[PASS * b : PASS * (b + 1), :].rearrange("(p t) m -> p t m", t=PACK)
+            nc.sync.dma_start(out=pages[i][:], in_=rows[:, t, :])
 
-        load_w(0, 0)
-        whalf = []
-        for hh in range(2):
-            w = two.tile([P, PACK, KP // 2], F32, name="whalf")
-            nc.sync.dma_start(
-                out=w[:], in_=wrelief[KP : 2 * KP, 256 * hh : 256 * (hh + 1)].rearrange("(p j) c -> p j c", j=PACK)
-            )
-            whalf.append(w)
-        wg0 = keep.tile([P, S], F32, name="wg0")
-        wg1 = keep.tile([P, PACK - 1, S], F32, name="wg1")
-        wgv = wgs.rearrange("(p t) j -> p t j", t=PACK)
-        for q in range(4):
-            nc.sync.dma_start(out=wg0[32 * q : 32 * q + 32], in_=wgv[:, 0, :])
-        nc.sync.dma_start(o2[:], offs2)
+        nc.sync.dma_start(pick[:], offs)
+        load_scale_rows(glare_sc_raw, wglare_scales)
+        tab_w = [load_table(0)]
+        load_scale_rows(tab_sc, tab_scales)
+        glare_raw = [load_glare_words("glare_first", 0, PASS)]
+        tab_w.append(load_table(1))
+        load_wrelief(0, 0)
+        whalves = []
+        for half in range(2):
+            whalf = two.tile([P, PACK, PASS // 2], F32, name="whalf")
+            nc.sync.dma_start(out=whalf[:], in_=wrelief_rows(1, PASS // 2 * half, PASS // 2 * (half + 1)))
+            whalves.append(whalf)
+        wgs_first = keep.tile([P, S], F32, name="wgs_first")
+        wgs_rest = keep.tile([P, PACK - 1, S], F32, name="wgs_rest")
+        wgs_rows = wgs.rearrange("(p t) j -> p t j", t=PACK)
+        for q in range(QUADRANTS):
+            nc.sync.dma_start(out=wgs_first[32 * q : 32 * (q + 1)], in_=wgs_rows[:, 0, :])
+        nc.sync.dma_start(slot[:], offs2)
         load_page(0)
-        for q in range(4):
-            nc.sync.dma_start(out=wg1[32 * q : 32 * q + 32], in_=wgv[:, 1:, :])
-        wg = [wg0[:]] + [wg1[:, t, :] for t in range(PACK - 1)]
-        nc.sync.dma_start(o3[:], offs3)
-        wr = keep.tile([P, NB, PACK], F32, name="wr")
-        nc.sync.dma_start(out=wr[:], in_=wear.rearrange("(b p t) -> p b t", p=P, t=PACK))
+        glare_rest = load_glare_words("glare_rest", PASS, H)
+        glare_raw.extend(glare_rest[:, :, PASS * b : PASS * (b + 1)] for b in range(GROUPS - 1))
+        for q in range(QUADRANTS):
+            nc.sync.dma_start(out=wgs_rest[32 * q : 32 * (q + 1)], in_=wgs_rows[:, 1:, :])
+        wgs_of = [wgs_first[:]] + [wgs_rest[:, t, :] for t in range(PACK - 1)]
+        nc.sync.dma_start(ref[:], offs3)
+        wear_sb = keep.tile([P, GROUPS, PACK], F32, name="wear_sb")
+        nc.sync.dma_start(out=wear_sb[:], in_=wear.rearrange("(b p t) -> p b t", p=P, t=PACK))
         load_page(1)
+        load_wrelief(1, 0)
+        load_wrelief(1, 1)
         load_page(2)
 
-        vw, vs = [], []
-        for a in range(NA):
-            w = keep.tile([P, S], U32, name=f"vw{a}", align_bytes=64)
-            nc.vector.tensor_copy(w[:], tw[a][:].bitcast(U32).indirect(o1[:]))
-            vw.append(w)
-        for a in range(NA):
-            s = keep.tile([P, S], U8, name=f"vs{a}", align_bytes=64)
-            nc.vector.tensor_copy(s[:], tsc[:, a, :].indirect(o1[:]))
-            vs.append(s)
+        v_words, v_scales = [], []
+        for a in range(K_PASSES):
+            words = keep.tile([P, S], U32, name=f"v_words{a}", align_bytes=64)
+            nc.vector.tensor_copy(words[:], tab_w[a][:].bitcast(U32).indirect(pick[:]))
+            v_words.append(words)
+        for a in range(K_PASSES):
+            scales = keep.tile([P, S], U8, name=f"v_scales{a}", align_bytes=64)
+            nc.vector.tensor_copy(scales[:], tab_sc[:, a, :].indirect(pick[:]))
+            v_scales.append(scales)
 
-        gw, gsc = {}, {}
+        glare_w, glare_sc = {}, {}
 
-        def deal_glare(b):
-            w = keep.tile([P, NA, PACK, 2 * P], U8, name=f"gw{b}", align_bytes=64)
-            sc = keep.tile([P, NA, PACK, P], U8, name=f"gsc{b}", align_bytes=64)
-            nc.scalar.copy(
-                out=w[:].bitcast(U16),
-                in_=gw_raw[:].bitcast(U16)[:, :, KP * b : KP * (b + 1)].rearrange("p a (q t) -> p a t q", t=PACK),
-            )
+        def move_glare_words(b):
+            glare_w[b] = keep.tile([P, K_PASSES, PACK, 2 * P], U8, name=f"glare_w{b}", align_bytes=64)
+            nc.scalar.copy(out=glare_w[b][:].bitcast(U16), in_=glare_raw[b].rearrange("p a (q t) -> p a t q", t=PACK))
+
+        for b in range(GROUPS):
+            glare_sc[b] = keep.tile([P, K_PASSES, PACK, P], U8, name=f"glare_sc{b}", align_bytes=64)
             nc.vector.tensor_copy(
-                out=sc[:], in_=gsc_raw[:, :, KP * b : KP * (b + 1)].rearrange("p a (q t) -> p a t q", t=PACK)
+                out=glare_sc[b][:],
+                in_=glare_sc_raw[:, :, PASS * b : PASS * (b + 1)].rearrange("p a (q t) -> p a t q", t=PACK),
             )
-            gw[b] = w
-            gsc[b] = sc
 
-        wcodes, wscales = {}, {}
+        relief_w, relief_sc = {}, {}
 
-        def prep_w(b, a, copy):
-            if a == 0:
-                wcodes[b] = two.tile([P, NA, KP], U32, name="wcodes", align_bytes=64)
-                wscales[b] = two.tile([P, NA, KP], U8, name="wscales", align_bytes=64)
-            wi = two.tile([P, PACK, P, PACK], BF16, name="wi", align_bytes=64)
-            copy(
-                out=wi[:].rearrange("p t m j -> p m j t"),
-                in_=wraw[b, a][:].rearrange("p j (m t) -> p m j t", t=PACK),
-            )
+        def round_wrelief(copy, woven, raw):
+            copy(out=woven.rearrange("p t q j -> p q j t"), in_=raw.rearrange("p j (q t) -> p q j t", t=PACK))
+
+        def quantise_wrelief_sets(b, a, woven, t0, t1):
             nc.vector.quantize_mx(
-                out=wcodes[b][:, a, :].bitcast(FP8X4),
-                scales=wscales[b][:, a, :],
-                in_=wi[:].rearrange("p t m j -> p (t m j)"),
+                out=relief_w[b][:, a, P * t0 : P * t1].bitcast(FP8X4),
+                scales=relief_sc[b][:, a, P * t0 : P * t1],
+                in_=woven[:, t0:t1].rearrange("p t q j -> p (t q j)"),
             )
 
-        damps, nums, gath = {}, {}, {}
+        def prepare_wrelief(b, a, copy):
+            if a == 0:
+                relief_w[b] = keep.tile([P, K_PASSES, PASS], U32, name="relief_w", tag=f"relief_w{b}", align_bytes=64)
+                relief_sc[b] = three.tile([P, K_PASSES, PASS], U8, name="relief_sc", align_bytes=64)
+            woven = keep.tile([P, PACK, P, PACK], BF16, name="wwoven", tag=f"wwoven{a}", align_bytes=64)
+            round_wrelief(copy, woven[:], wraw[b, a][:])
+            quantise_wrelief_sets(b, a, woven, 0, PACK)
 
-        def glare(i):
-            b, t = divmod(i, PACK)
-            bank = psum.tile([P, S], F32, name="bank", tag="bank")
-            for a in range(NA):
+        damps, nums, fetched = {}, {}, {}
+
+        def first_product(bank_index, words, scales, dtype):
+            bank = psum.tile([P, S], F32, name="bank", tag=f"bank{bank_index}")
+            for a in range(K_PASSES):
                 nc.tensor.matmul_mx(
                     out=bank[:],
-                    lhsT=gw[b][:, a, t, :].bitcast(FP4X4),
-                    lhsT_scale=gsc[b][:, a, t, :],
-                    rhs=vw[a][:].bitcast(FP8X4),
-                    rhs_scale=vs[a][:],
+                    lhsT=words(a).bitcast(dtype),
+                    lhsT_scale=scales(a),
+                    rhs=v_words[a][:].bitcast(FP8X4),
+                    rhs_scale=v_scales[a][:],
                     start=(a == 0),
-                    stop=(a == NA - 1),
+                    stop=(a == K_PASSES - 1),
                 )
-            mag = keep.tile([P, S], F32, name="mag", tag=f"m{i % 2}")
+            return bank
+
+        def damping(i):
+            b, t = divmod(i, PACK)
+            bank = first_product(
+                PACK * (b % 2) + t, lambda a: glare_w[b][:, a, t, :], lambda a: glare_sc[b][:, a, t, :], FP4X4
+            )
+            mag = keep.tile([P, S], F32, name="mag", tag=f"mag{i % 2}", align_bytes=64)
             nc.scalar.activation(out=mag[:], in_=bank[:], func=ACT.Abs)
-            root = keep.tile([P, S], F32, name="root", tag=f"r{i % 4}")
+            root = keep.tile([P, S], F32, name="root", tag=f"root{i % PACK}")
             nc.scalar.activation(out=root[:], in_=mag[:], func=ACT.Abs_reciprocal_sqrt, bias=1.0)
-            d = damp.tile([P, S], F32, name="d")
-            nc.scalar.activation(out=d[:], in_=root[:], func=ACT.Square)
-            damps[i] = d
+            if i < EARLY_SETS:
+                damps[i] = keep.tile([P, S], F32, name="damp", tag=("early0", "relief_w1", "early1")[i], align_bytes=64)
+            else:
+                damps[i] = damp_pool.tile([P, S], F32, name="damp")
+            nc.scalar.activation(out=damps[i][:], in_=root[:], func=ACT.Square)
 
-        def relief(i):
+        def numerator(i):
             b, t = divmod(i, PACK)
-            bank = psum.tile([P, S], F32, name="bank", tag="bank")
-            for a in range(NA):
-                nc.tensor.matmul_mx(
-                    out=bank[:],
-                    lhsT=wcodes[b][:, a, P * t : P * (t + 1)].bitcast(FP8X4),
-                    lhsT_scale=wscales[b][:, a, P * t : P * (t + 1)],
-                    rhs=vw[a][:].bitcast(FP8X4),
-                    rhs_scale=vs[a][:],
-                    start=(a == 0),
-                    stop=(a == NA - 1),
-                )
-            n = keep.tile([P, S], F32, name="num", tag=f"r{(i - 1) % 4}")
-            nc.vector.tensor_tensor(out=n[:], in0=bank[:], in1=wg[t], op=ALU.mult)
-            nums[i] = n
+            cols = slice(P * t, P * (t + 1))
+            bank = first_product(
+                PACK * ((b + 1) % 2) + t, lambda a: relief_w[b][:, a, cols], lambda a: relief_sc[b][:, a, cols], FP8X4
+            )
+            if 1 <= i <= EARLY_SETS:
+                nums[i] = keep.tile([P, S], F32, name="num", tag=("early0", "early0", "early1")[i - 1], align_bytes=64)
+            else:
+                nums[i] = keep.tile([P, S], F32, name="num", tag=f"root{(i - 1) % PACK}")
+            nc.vector.tensor_tensor(out=nums[i][:], in0=bank[:], in1=wgs_of[t], op=ALU.mult)
 
         def put(i):
-            nc.vector.tensor_tensor(out=pages[i][:].indirect(o2[:]), in0=nums[i][:], in1=damps[i][:], op=ALU.mult)
+            nc.vector.tensor_tensor(out=pages[i][:].indirect(slot[:]), in0=nums[i][:], in1=damps[i][:], op=ALU.mult)
 
         def fetch(i):
-            g = keep.tile([P, NX], F32, name="g", tag=f"g{i % 2}")
-            nc.vector.tensor_copy(g[:], pages[i][:].indirect(o3[:]))
-            gath[i] = g
+            fetched[i] = keep.tile([P, NX], F32, name="fetched", tag=f"fetched{i % 2}")
+            nc.vector.tensor_copy(fetched[i][:], pages[i][:].indirect(ref[:]))
 
-        pplanes, xplanes = {}, {}
+        page_bf, x_bf = {}, {}
 
         def round_page(i):
             b, t = divmod(i, PACK)
             if t == 0:
-                pplanes[b] = two.tile([P, PACK, T2], BF16, name="pplanes")
-            nc.gpsimd.tensor_scalar(
-                out=pplanes[b][:, t, :], in0=pages[i][:], scalar1=1.0, scalar2=0.0, op0=ALU.mult, op1=ALU.add
-            )
+                page_bf[b] = two.tile([P, PACK, T2], BF16, name="page_bf")
+            nc.scalar.copy(out=page_bf[b][:, t, :], in_=pages[i][:])
 
-        def round_rows(i):
+        def round_x_columns(i, xmag, cols):
+            b, t = divmod(i, PACK)
+            nc.scalar.activation(out=xmag[:, cols], in_=fetched[i][:, cols], func=ACT.Abs)
+            nc.scalar.activation(out=x_bf[b][:, t, cols], in_=xmag[:, cols], func=ACT.Copy, scale=wear_sb[:, b, t : t + 1])
+
+        def round_x(i):
             b, t = divmod(i, PACK)
             if t == 0:
-                xplanes[b] = two.tile([P, PACK, NX], BF16, name="xplanes")
-            ga = keep.tile([P, NX], F32, name="ga", tag=f"m{(i + 1) % 2}")
-            nc.scalar.activation(out=ga[:], in_=gath[i][:], func=ACT.Abs)
-            nc.scalar.activation(out=xplanes[b][:, t, :], in_=ga[:], func=ACT.Copy, scale=wr[:, b, t : t + 1])
+                x_bf[b] = two.tile([P, PACK, NX], BF16, name="x_bf")
+            tag = f"wwoven{i}" if i < K_PASSES else f"mag{(i + 1) % 2}"
+            xmag = keep.tile([P, NX], F32, name="xmag", tag=tag, align_bytes=64)
+            round_x_columns(i, xmag, slice(0, NX))
 
-        pcodes = [[keep.tile([P, KP], U32, name=f"pc{b}{hh}", align_bytes=64) for hh in range(2)] for b in range(NB)]
-        pscales = [[keep.tile([P, KP], U8, name=f"ps{b}{hh}", align_bytes=64) for hh in range(2)] for b in range(NB)]
-        xcodes = [keep.tile([P, NX], U32, name=f"xc{b}", align_bytes=64) for b in range(NB)]
-        xscales = [keep.tile([P, NX], U8, name=f"xs{b}", align_bytes=64) for b in range(NB)]
+        def operand_tiles(name, dtype):
+            return keep.tile([P, PASS], dtype, name=name, align_bytes=64)
 
-        def weave(dst, planes, c0, c1, d0, copy):
+        page_w = [[operand_tiles(f"page_w{b}{half}", U32) for half in range(2)] for b in range(GROUPS)]
+        page_sc = [[operand_tiles(f"page_sc{b}{half}", U8) for half in range(2)] for b in range(GROUPS)]
+        x_w = [operand_tiles(f"x_w{b}", U32) for b in range(GROUPS)]
+        x_sc = [operand_tiles(f"x_sc{b}", U8) for b in range(GROUPS)]
+
+        def weave(copy, woven, rows, c0, c1):
             copy(
-                out=dst[:, d0 : d0 + c1 - c0, :].rearrange("p (c i) t -> p c t i", i=4),
-                in_=planes[:, :, c0:c1].rearrange("p t (c i) -> p c t i", i=4),
+                out=woven.rearrange("p (c i) t -> p c t i", i=RUN),
+                in_=rows[:, :, c0:c1].rearrange("p t (c i) -> p c t i", i=RUN),
             )
 
-        def quant(src, codes, scales):
-            nc.vector.quantize_mx(out=codes.bitcast(FP8X4), scales=scales, in_=src[:].rearrange("p c t -> p (c t)"))
+        def quantise(woven, words, scales):
+            nc.vector.quantize_mx(out=words.bitcast(FP8X4), scales=scales, in_=woven[:].rearrange("p c t -> p (c t)"))
 
-        def page_half(b, hh, copy):
-            wv = three.tile([P, KP, PACK], BF16, name="wv", align_bytes=64)
-            weave(wv, pplanes[b], KP * hh, KP * (hh + 1), 0, copy)
-            quant(wv, pcodes[b][hh][:], pscales[b][hh][:])
+        def page_half(b, half):
+            woven = three.tile([P, PASS, PACK], BF16, name="woven", align_bytes=64)
+            weave(nc.scalar.copy, woven[:], page_bf[b], PASS * half, PASS * (half + 1))
+            quantise(woven, page_w[b][half][:], page_sc[b][half][:])
 
         def x_group(b):
-            wv = three.tile([P, KP, PACK], BF16, name="wv", align_bytes=64)
-            weave(wv, xplanes[b], 0, NX, 0, nc.scalar.copy)
-            quant(wv, xcodes[b][:], xscales[b][:])
+            woven = three.tile([P, PASS, PACK], BF16, name="woven", align_bytes=64)
+            weave(nc.scalar.copy, woven[:], x_bf[b], 0, NX)
+            quantise(woven, x_w[b][:], x_sc[b][:])
 
-        deal_glare(0)
-        glare(0)
-        prep_w(0, 0, nc.vector.tensor_copy)
-        wi = two.tile([P, PACK, P, PACK], BF16, name="wi", align_bytes=64)
-        for hh in range(2):
-            nc.vector.tensor_copy(
-                out=wi[:, :, 64 * hh : 64 * (hh + 1), :].rearrange("p t m j -> p m j t"),
-                in_=whalf[hh][:].rearrange("p j (m t) -> p m j t", t=PACK),
-            )
-        for t0, t1 in ((0, 1), (1, PACK)):
-            nc.vector.quantize_mx(
-                out=wcodes[0][:, 1, P * t0 : P * t1].bitcast(FP8X4),
-                scales=wscales[0][:, 1, P * t0 : P * t1],
-                in_=wi[:, t0:t1].rearrange("p t m j -> p (t m j)"),
-            )
-        relief(0)
-        deal_glare(1)
-        deal_glare(2)
+        move_glare_words(0)
+        prepare_wrelief(0, 0, nc.vector.tensor_copy)
+        damping(0)
+        wwoven = keep.tile([P, PACK, P, PACK], BF16, name="wwoven", tag="wwoven1", align_bytes=64)
+        for half in range(2):
+            round_wrelief(nc.vector.tensor_copy, wwoven[:, :, P // 2 * half : P // 2 * (half + 1), :], whalves[half][:])
+        quantise_wrelief_sets(0, 1, wwoven, 0, 1)
+        quantise_wrelief_sets(0, 1, wwoven, 1, PACK)
+        numerator(0)
+        damping(1)
+        move_glare_words(1)
+        move_glare_words(2)
+
         lims = []
-        for i in range(NT):
-            b, t = divmod(i, PACK)
-            if i + 3 < NT:
-                load_page(i + 3)
-            if i < 4:
-                load_w(1 + i // 2, i % 2)
-            if i == 2 * PACK:
-                for hh in range(2):
-                    lm = big.tile([P, NM // 2, NX], F32, name="lm", tag="big", align_bytes=64)
-                    nc.sync.dma_start(out=lm[:], in_=lim[KP * hh : KP * (hh + 1), :].rearrange("(c p) j -> p c j", p=P))
-                    lims.append(lm)
-            if i >= 1:
-                glare(i)
-            put(i)
-            round_page(i)
-            if i + 1 < NT:
-                relief(i + 1)
+        for i in range(SETS):
+            if i + PAGES_AHEAD < SETS:
+                load_page(i + PAGES_AHEAD)
+            if i < K_PASSES:
+                load_wrelief(GROUPS - 1, i)
+            if i == SETS - PACK:
+                for half in range(2):
+                    lim_half = big.tile([P, OUT_TILES // 2, NX], F32, name="lim_half", tag="big", align_bytes=64)
+                    rows = lim[T2 // 2 * half : T2 // 2 * (half + 1), :]
+                    nc.sync.dma_start(out=lim_half[:], in_=rows.rearrange("(c p) j -> p c j", p=P))
+                    lims.append(lim_half)
             if i >= 2:
-                round_rows(i - 2)
-            if i < NT - 1:
+                damping(i)
+            put(i)
+            if i + 1 < SETS:
+                numerator(i + 1)
+            if i >= ROUND_LAG:
+                round_x(i - ROUND_LAG)
+                round_page(i - ROUND_LAG)
+            if i + 1 < SETS:
                 fetch(i)
-            if 1 <= i <= 4:
-                prep_w(1 + (i - 1) // 2, (i - 1) % 2, nc.scalar.copy)
-            if i in (5, 6):
-                page_half(0, i - 5, nc.scalar.copy)
-            if i in (8, 9):
-                page_half(1, i - 8, nc.scalar.copy)
-            if i in (7, 10):
-                x_group((i - 7) // 3)
+            if i < K_PASSES * (GROUPS - 1):
+                prepare_wrelief(1 + i // K_PASSES, i % K_PASSES, nc.scalar.copy)
+            for b in range(GROUPS - 1):
+                since_rounded = i - (PACK * b + PACK - 1 + ROUND_LAG)
+                if since_rounded in (0, 1):
+                    page_half(b, since_rounded)
+                if since_rounded == (2, 0)[b]:
+                    x_group(b)
+
         def score_pass(bank, m, b):
+            half, cols = m // PACK, slice(P * (m % PACK), P * (m % PACK + 1))
             nc.tensor.matmul_mx(
                 out=bank[:],
-                lhsT=pcodes[b][m // 4][:, P * (m % 4) : P * (m % 4 + 1)].bitcast(FP8X4),
-                lhsT_scale=pscales[b][m // 4][:, P * (m % 4) : P * (m % 4 + 1)],
-                rhs=xcodes[b][:].bitcast(FP8X4),
-                rhs_scale=xscales[b][:],
+                lhsT=page_w[b][half][:, cols].bitcast(FP8X4),
+                lhsT_scale=page_sc[b][half][:, cols],
+                rhs=x_w[b][:].bitcast(FP8X4),
+                rhs_scale=x_sc[b][:],
                 start=(b == 0),
-                stop=(b == NB - 1),
+                stop=(b == GROUPS - 1),
             )
 
         banks = []
-        for m in range(NM):
-            bank = psum.tile([P, NX], F32, name="bank", tag="bank")
+        for m in range(OUT_TILES):
+            bank = psum.tile([P, NX], F32, name="bank", tag=f"bank{PACK * ((m + 1) % 2) + m // 2}")
             score_pass(bank, m, 0)
             banks.append(bank)
-        for m in range(NM):
+        for m in range(OUT_TILES):
             score_pass(banks[m], m, 1)
-        round_rows(NT - 2)
-        last = NT - 1
-        Q = 256
-        g = keep.tile([P, NX], F32, name="g", tag=f"g{last % 2}")
-        ga = keep.tile([P, NX], F32, name="ga", tag=f"m{(last + 1) % 2}")
-        for hh in range(2):
-            cols = slice(Q * hh, Q * (hh + 1))
-            nc.vector.tensor_copy(g[:, cols], pages[last][:].indirect(o3[:, 16 * hh : 16 * (hh + 1)]))
-            nc.scalar.activation(out=ga[:, cols], in_=g[:, cols], func=ACT.Abs)
-            nc.scalar.activation(
-                out=xplanes[NB - 1][:, PACK - 1, cols], in_=ga[:, cols], func=ACT.Copy, scale=wr[:, NB - 1, PACK - 1 : PACK]
-            )
 
-        def quarter(planes, c0, copy):
-            wq = keep.tile([P, Q, PACK], BF16, name="wq", tag=f"wq{len(quarters)}", align_bytes=64)
-            weave(wq, planes, c0, c0 + Q, 0, copy)
-            quarters.append(wq)
-            return wq
+        last, last_b = SETS - 1, GROUPS - 1
+        round_x(last - 1)
+        round_page(last - 1)
+        fetched[last] = keep.tile([P, NX], F32, name="fetched", tag=f"fetched{last % 2}")
+        xmag_last = keep.tile([P, NX], F32, name="xmag", tag=f"mag{(last + 1) % 2}", align_bytes=64)
+        nc.scalar.copy(out=page_bf[last_b][:, PACK - 1, 0 : T2 // 2], in_=pages[last][:, 0 : T2 // 2])
+        for half in range(2):
+            cols = slice(QUARTER * half, QUARTER * (half + 1))
+            entries = ref[:, QUARTER // LIST_ROWS * half : QUARTER // LIST_ROWS * (half + 1)]
+            nc.vector.tensor_copy(fetched[last][:, cols], pages[last][:].indirect(entries))
+            round_x_columns(last, xmag_last, cols)
 
-        def quant_page_quarter(k, wq):
-            cols = slice(Q * (k % 2), Q * (k % 2 + 1))
-            quant(wq, pcodes[NB - 1][k // 2][:, cols], pscales[NB - 1][k // 2][:, cols])
+        def weave_page_quarter(k, copy):
+            woven = keep.tile([P, QUARTER, PACK], BF16, name=f"quarter{k}", align_bytes=64)
+            weave(copy, woven[:], page_bf[last_b], QUARTER * k, QUARTER * (k + 1))
+            return woven
 
-        quarters = []
-        p0 = quarter(pplanes[NB - 1], 0, nc.vector.tensor_copy)
-        xa = quarter(xplanes[NB - 1], 0, nc.vector.tensor_copy)
-        xb = quarter(xplanes[NB - 1], Q, nc.scalar.copy)
-        quant_page_quarter(0, p0)
-        quant(xa, xcodes[NB - 1][:, 0:Q], xscales[NB - 1][:, 0:Q])
-        quant(xb, xcodes[NB - 1][:, Q:], xscales[NB - 1][:, Q:])
+        def quantise_page_quarter(k, woven):
+            cols = slice(QUARTER * (k % 2), QUARTER * (k % 2 + 1))
+            quantise(woven, page_w[last_b][k // 2][:, cols], page_sc[last_b][k // 2][:, cols])
 
-        for m in range(NM):
-            if m % 2 == 0 and m + 2 < NM:
-                quant_page_quarter(m // 2 + 1, quarter(pplanes[NB - 1], Q * (m // 2 + 1), nc.scalar.copy))
-            score_pass(banks[m], m, NB - 1)
-            res = lims[m // 4][:, m % 4, :]
-            nc.vector.tensor_tensor(out=res, in0=banks[m][:], in1=res, op=ALU.max)
-            nc.sync.dma_start(out=out[P * m : P * (m + 1), :], in_=res)
+        first_quarter = weave_page_quarter(0, nc.vector.tensor_copy)
+        x_woven = three.tile([P, PASS, PACK], BF16, name="woven", align_bytes=64)
+        for c0, c1, copy in (
+            (0, QUARTER, nc.vector.tensor_copy),
+            (QUARTER, X_ON_VECTOR, nc.vector.tensor_copy),
+            (X_ON_VECTOR, NX, nc.scalar.copy),
+        ):
+            weave(copy, x_woven[:, c0:c1, :], x_bf[last_b], c0, c1)
+        quantise_page_quarter(0, first_quarter)
+        quantise(x_woven, x_w[last_b][:], x_sc[last_b][:])
+        nc.scalar.copy(out=page_bf[last_b][:, PACK - 1, T2 // 2 :], in_=pages[last][:, T2 // 2 :])
+
+        for m in range(OUT_TILES):
+            if m % 2 == 0 and m + 2 < OUT_TILES:
+                quantise_page_quarter(m // 2 + 1, weave_page_quarter(m // 2 + 1, nc.scalar.copy))
+            score_pass(banks[m], m, last_b)
+            result = lims[m // PACK][:, m % PACK, :]
+            nc.vector.tensor_tensor(out=result, in0=banks[m][:], in1=result, op=ALU.max)
+            nc.sync.dma_start(out=out[P * m : P * (m + 1), :], in_=result)

from contextlib import ExitStack

import concourse.mybir as mybir

K, H, T, S, T2, NX = 1024, 1536, 2048, 512, 1024, 512
FLOPS = 2 * (2 * K * H * S + H * T2 * NX)

F32 = mybir.dt.float32
BF16 = mybir.dt.bfloat16
I32 = mybir.dt.int32
U32 = mybir.dt.uint32
U16 = mybir.dt.uint16
U8 = mybir.dt.uint8
FP8X4 = mybir.dt.float8_e4m3fn_x4
FP4X4 = mybir.dt.float4_e2m1fn_x4
ACT = mybir.ActivationFunctionType
ALU = mybir.AluOpType

P = 128
PACK = 4
PASS = P * PACK
K_PASSES = K // PASS
GROUPS = H // PASS
SETS = GROUPS * PACK
OUT_TILES = T2 // P
QUADRANTS = 4
SCALE_ROWS = 4
LIST_ROWS = 16
RUN = 4
QUARTER = T2 // 4
X_ON_VECTOR = 384
PAGES_AHEAD = 3
ROUND_LAG = 2
EARLY_SETS = 3


def tile_list_die_wear_match_kernel(
    tc, tab_words, tab_scales, offs, offs2, offs3, wrelief, wglare_words, wglare_scales, page0, wgs, wear, lim, out
):
    nc = tc.nc
    with ExitStack() as ctx:
        keep = ctx.enter_context(tc.tile_pool(name="keep", bufs=1))
        big = ctx.enter_context(tc.tile_pool(name="big", bufs=2))
        wraw_pool = ctx.enter_context(tc.tile_pool(name="wraw", bufs=3))
        two = ctx.enter_context(tc.tile_pool(name="two", bufs=2))
        three = ctx.enter_context(tc.tile_pool(name="three", bufs=3))
        damp_pool = ctx.enter_context(tc.tile_pool(name="damp", bufs=3))
        page_pool = ctx.enter_context(tc.tile_pool(name="pages", bufs=PAGES_AHEAD + ROUND_LAG + 1))
        psum = ctx.enter_context(tc.psum_pool(name="psum", bufs=1))

        pick = keep.tile([P, S // LIST_ROWS], U16, name="pick")
        slot = keep.tile([P, S // LIST_ROWS], U16, name="slot")
        ref = keep.tile([P, NX // LIST_ROWS], U16, name="ref")
        tab_sc = keep.tile([P, K_PASSES, T], U8, name="tab_sc", align_bytes=64)
        glare_sc_raw = keep.tile([P, K_PASSES, H], U8, name="glare_sc_raw", align_bytes=64)
        nc.vector.memset(glare_sc_raw[:].bitcast(I32), 0)
        nc.vector.memset(tab_sc[:].bitcast(I32), 0)

        def load_scale_rows(dst, scales):
            for q in range(QUADRANTS):
                nc.sync.dma_start(
                    out=dst[32 * q : 32 * q + SCALE_ROWS].bitcast(I32),
                    in_=scales[:, SCALE_ROWS * q : SCALE_ROWS * (q + 1), :].rearrange("a r c -> r a c").bitcast(I32),
                )

        def load_table(a):
            words = big.tile([P, T], I32, name="tab_w", tag="big", align_bytes=64)
            nc.sync.dma_start(out=words[:], in_=tab_words[a].rearrange("p t i -> p (t i)").bitcast(I32))
            return words

        def load_glare_words(name, c0, c1):
            raw = keep.tile([P, K_PASSES, 2 * (c1 - c0)], U8, name=name, align_bytes=64)
            nc.sync.dma_start(
                out=raw[:].bitcast(I32), in_=wglare_words.rearrange("a p c -> p a c")[:, :, 2 * c0 : 2 * c1].bitcast(I32)
            )
            return raw[:].bitcast(U16)

        def wrelief_rows(a, c0, c1):
            return wrelief[PASS * a : PASS * (a + 1), c0:c1].rearrange("(p j) c -> p j c", j=PACK)

        wraw, pages = {}, {}

        def load_wrelief(b, a):
            wraw[b, a] = wraw_pool.tile([P, PACK, PASS], F32, name="wraw")
            nc.sync.dma_start(out=wraw[b, a][:], in_=wrelief_rows(a, PASS * b, PASS * (b + 1)))

        def load_page(i):
            b, t = divmod(i, PACK)
            pages[i] = page_pool.tile([P, T2], F32, name="page")
            rows = page0[PASS * b : PASS * (b + 1), :].rearrange("(p t) m -> p t m", t=PACK)
            nc.sync.dma_start(out=pages[i][:], in_=rows[:, t, :])

        nc.sync.dma_start(pick[:], offs)
        load_scale_rows(glare_sc_raw, wglare_scales)
        tab_w = [load_table(0)]
        load_scale_rows(tab_sc, tab_scales)
        glare_raw = [load_glare_words("glare_first", 0, PASS)]
        tab_w.append(load_table(1))
        load_wrelief(0, 0)
        whalves = []
        for half in range(2):
            whalf = two.tile([P, PACK, PASS // 2], F32, name="whalf")
            nc.sync.dma_start(out=whalf[:], in_=wrelief_rows(1, PASS // 2 * half, PASS // 2 * (half + 1)))
            whalves.append(whalf)
        wgs_first = keep.tile([P, S], F32, name="wgs_first")
        wgs_rest = keep.tile([P, PACK - 1, S], F32, name="wgs_rest")
        wgs_rows = wgs.rearrange("(p t) j -> p t j", t=PACK)
        for q in range(QUADRANTS):
            nc.sync.dma_start(out=wgs_first[32 * q : 32 * (q + 1)], in_=wgs_rows[:, 0, :])
        nc.sync.dma_start(slot[:], offs2)
        load_page(0)
        glare_rest = load_glare_words("glare_rest", PASS, H)
        glare_raw.extend(glare_rest[:, :, PASS * b : PASS * (b + 1)] for b in range(GROUPS - 1))
        for q in range(QUADRANTS):
            nc.sync.dma_start(out=wgs_rest[32 * q : 32 * (q + 1)], in_=wgs_rows[:, 1:, :])
        wgs_of = [wgs_first[:]] + [wgs_rest[:, t, :] for t in range(PACK - 1)]
        nc.sync.dma_start(ref[:], offs3)
        wear_sb = keep.tile([P, GROUPS, PACK], F32, name="wear_sb")
        nc.sync.dma_start(out=wear_sb[:], in_=wear.rearrange("(b p t) -> p b t", p=P, t=PACK))
        load_page(1)
        load_wrelief(1, 0)
        load_wrelief(1, 1)
        load_page(2)

        v_words, v_scales = [], []
        for a in range(K_PASSES):
            words = keep.tile([P, S], U32, name=f"v_words{a}", align_bytes=64)
            nc.vector.tensor_copy(words[:], tab_w[a][:].bitcast(U32).indirect(pick[:]))
            v_words.append(words)
        for a in range(K_PASSES):
            scales = keep.tile([P, S], U8, name=f"v_scales{a}", align_bytes=64)
            nc.vector.tensor_copy(scales[:], tab_sc[:, a, :].indirect(pick[:]))
            v_scales.append(scales)

        glare_w, glare_sc = {}, {}

        def move_glare_words(b):
            glare_w[b] = keep.tile([P, K_PASSES, PACK, 2 * P], U8, name=f"glare_w{b}", align_bytes=64)
            nc.scalar.copy(out=glare_w[b][:].bitcast(U16), in_=glare_raw[b].rearrange("p a (q t) -> p a t q", t=PACK))

        for b in range(GROUPS):
            glare_sc[b] = keep.tile([P, K_PASSES, PACK, P], U8, name=f"glare_sc{b}", align_bytes=64)
            nc.vector.tensor_copy(
                out=glare_sc[b][:],
                in_=glare_sc_raw[:, :, PASS * b : PASS * (b + 1)].rearrange("p a (q t) -> p a t q", t=PACK),
            )

        relief_w, relief_sc = {}, {}

        def round_wrelief(copy, woven, raw):
            copy(out=woven.rearrange("p t q j -> p q j t"), in_=raw.rearrange("p j (q t) -> p q j t", t=PACK))

        def quantise_wrelief_sets(b, a, woven, t0, t1):
            nc.vector.quantize_mx(
                out=relief_w[b][:, a, P * t0 : P * t1].bitcast(FP8X4),
                scales=relief_sc[b][:, a, P * t0 : P * t1],
                in_=woven[:, t0:t1].rearrange("p t q j -> p (t q j)"),
            )

        def prepare_wrelief(b, a, copy):
            if a == 0:
                relief_w[b] = keep.tile([P, K_PASSES, PASS], U32, name="relief_w", tag=f"relief_w{b}", align_bytes=64)
                relief_sc[b] = three.tile([P, K_PASSES, PASS], U8, name="relief_sc", align_bytes=64)
            woven = keep.tile([P, PACK, P, PACK], BF16, name="wwoven", tag=f"wwoven{a}", align_bytes=64)
            round_wrelief(copy, woven[:], wraw[b, a][:])
            quantise_wrelief_sets(b, a, woven, 0, PACK)

        damps, nums, fetched = {}, {}, {}

        def first_product(bank_index, words, scales, dtype):
            bank = psum.tile([P, S], F32, name="bank", tag=f"bank{bank_index}")
            for a in range(K_PASSES):
                nc.tensor.matmul_mx(
                    out=bank[:],
                    lhsT=words(a).bitcast(dtype),
                    lhsT_scale=scales(a),
                    rhs=v_words[a][:].bitcast(FP8X4),
                    rhs_scale=v_scales[a][:],
                    start=(a == 0),
                    stop=(a == K_PASSES - 1),
                )
            return bank

        def damping(i):
            b, t = divmod(i, PACK)
            bank = first_product(
                PACK * (b % 2) + t, lambda a: glare_w[b][:, a, t, :], lambda a: glare_sc[b][:, a, t, :], FP4X4
            )
            mag = keep.tile([P, S], F32, name="mag", tag=f"mag{i % 2}", align_bytes=64)
            nc.scalar.activation(out=mag[:], in_=bank[:], func=ACT.Abs)
            root = keep.tile([P, S], F32, name="root", tag=f"root{i % PACK}")
            nc.scalar.activation(out=root[:], in_=mag[:], func=ACT.Abs_reciprocal_sqrt, bias=1.0)
            if i < EARLY_SETS:
                damps[i] = keep.tile([P, S], F32, name="damp", tag=("early0", "relief_w1", "early1")[i], align_bytes=64)
            else:
                damps[i] = damp_pool.tile([P, S], F32, name="damp")
            nc.scalar.activation(out=damps[i][:], in_=root[:], func=ACT.Square)

        def numerator(i):
            b, t = divmod(i, PACK)
            cols = slice(P * t, P * (t + 1))
            bank = first_product(
                PACK * ((b + 1) % 2) + t, lambda a: relief_w[b][:, a, cols], lambda a: relief_sc[b][:, a, cols], FP8X4
            )
            if 1 <= i <= EARLY_SETS:
                nums[i] = keep.tile([P, S], F32, name="num", tag=("early0", "early0", "early1")[i - 1], align_bytes=64)
            else:
                nums[i] = keep.tile([P, S], F32, name="num", tag=f"root{(i - 1) % PACK}")
            nc.vector.tensor_tensor(out=nums[i][:], in0=bank[:], in1=wgs_of[t], op=ALU.mult)

        def put(i):
            nc.vector.tensor_tensor(out=pages[i][:].indirect(slot[:]), in0=nums[i][:], in1=damps[i][:], op=ALU.mult)

        def fetch(i):
            fetched[i] = keep.tile([P, NX], F32, name="fetched", tag=f"fetched{i % 2}")
            nc.vector.tensor_copy(fetched[i][:], pages[i][:].indirect(ref[:]))

        page_bf, x_bf = {}, {}

        def round_page(i):
            b, t = divmod(i, PACK)
            if t == 0:
                page_bf[b] = two.tile([P, PACK, T2], BF16, name="page_bf")
            nc.scalar.copy(out=page_bf[b][:, t, :], in_=pages[i][:])

        def round_x_columns(i, xmag, cols):
            b, t = divmod(i, PACK)
            nc.scalar.activation(out=xmag[:, cols], in_=fetched[i][:, cols], func=ACT.Abs)
            nc.scalar.activation(out=x_bf[b][:, t, cols], in_=xmag[:, cols], func=ACT.Copy, scale=wear_sb[:, b, t : t + 1])

        def round_x(i):
            b, t = divmod(i, PACK)
            if t == 0:
                x_bf[b] = two.tile([P, PACK, NX], BF16, name="x_bf")
            tag = f"wwoven{i}" if i < K_PASSES else f"mag{(i + 1) % 2}"
            xmag = keep.tile([P, NX], F32, name="xmag", tag=tag, align_bytes=64)
            round_x_columns(i, xmag, slice(0, NX))

        def operand_tiles(name, dtype):
            return keep.tile([P, PASS], dtype, name=name, align_bytes=64)

        page_w = [[operand_tiles(f"page_w{b}{half}", U32) for half in range(2)] for b in range(GROUPS)]
        page_sc = [[operand_tiles(f"page_sc{b}{half}", U8) for half in range(2)] for b in range(GROUPS)]
        x_w = [operand_tiles(f"x_w{b}", U32) for b in range(GROUPS)]
        x_sc = [operand_tiles(f"x_sc{b}", U8) for b in range(GROUPS)]

        def weave(copy, woven, rows, c0, c1):
            copy(
                out=woven.rearrange("p (c i) t -> p c t i", i=RUN),
                in_=rows[:, :, c0:c1].rearrange("p t (c i) -> p c t i", i=RUN),
            )

        def quantise(woven, words, scales):
            nc.vector.quantize_mx(out=words.bitcast(FP8X4), scales=scales, in_=woven[:].rearrange("p c t -> p (c t)"))

        def page_half(b, half):
            woven = three.tile([P, PASS, PACK], BF16, name="woven", align_bytes=64)
            weave(nc.scalar.copy, woven[:], page_bf[b], PASS * half, PASS * (half + 1))
            quantise(woven, page_w[b][half][:], page_sc[b][half][:])

        def x_group(b):
            woven = three.tile([P, PASS, PACK], BF16, name="woven", align_bytes=64)
            weave(nc.scalar.copy, woven[:], x_bf[b], 0, NX)
            quantise(woven, x_w[b][:], x_sc[b][:])

        move_glare_words(0)
        prepare_wrelief(0, 0, nc.vector.tensor_copy)
        damping(0)
        wwoven = keep.tile([P, PACK, P, PACK], BF16, name="wwoven", tag="wwoven1", align_bytes=64)
        for half in range(2):
            round_wrelief(nc.vector.tensor_copy, wwoven[:, :, P // 2 * half : P // 2 * (half + 1), :], whalves[half][:])
        quantise_wrelief_sets(0, 1, wwoven, 0, 1)
        quantise_wrelief_sets(0, 1, wwoven, 1, PACK)
        numerator(0)
        damping(1)
        move_glare_words(1)
        move_glare_words(2)

        lims = []
        for i in range(SETS):
            if i + PAGES_AHEAD < SETS:
                load_page(i + PAGES_AHEAD)
            if i < K_PASSES:
                load_wrelief(GROUPS - 1, i)
            if i == SETS - PACK:
                for half in range(2):
                    lim_half = big.tile([P, OUT_TILES // 2, NX], F32, name="lim_half", tag="big", align_bytes=64)
                    rows = lim[T2 // 2 * half : T2 // 2 * (half + 1), :]
                    nc.sync.dma_start(out=lim_half[:], in_=rows.rearrange("(c p) j -> p c j", p=P))
                    lims.append(lim_half)
            if i >= 2:
                damping(i)
            put(i)
            if i + 1 < SETS:
                numerator(i + 1)
            if i >= ROUND_LAG:
                round_x(i - ROUND_LAG)
                round_page(i - ROUND_LAG)
            if i + 1 < SETS:
                fetch(i)
            if i < K_PASSES * (GROUPS - 1):
                prepare_wrelief(1 + i // K_PASSES, i % K_PASSES, nc.scalar.copy)
            for b in range(GROUPS - 1):
                since_rounded = i - (PACK * b + PACK - 1 + ROUND_LAG)
                if since_rounded in (0, 1):
                    page_half(b, since_rounded)
                if since_rounded == (2, 0)[b]:
                    x_group(b)

        def score_pass(bank, m, b):
            half, cols = m // PACK, slice(P * (m % PACK), P * (m % PACK + 1))
            nc.tensor.matmul_mx(
                out=bank[:],
                lhsT=page_w[b][half][:, cols].bitcast(FP8X4),
                lhsT_scale=page_sc[b][half][:, cols],
                rhs=x_w[b][:].bitcast(FP8X4),
                rhs_scale=x_sc[b][:],
                start=(b == 0),
                stop=(b == GROUPS - 1),
            )

        banks = []
        for m in range(OUT_TILES):
            bank = psum.tile([P, NX], F32, name="bank", tag=f"bank{PACK * ((m + 1) % 2) + m // 2}")
            score_pass(bank, m, 0)
            banks.append(bank)
        for m in range(OUT_TILES):
            score_pass(banks[m], m, 1)

        last, last_b = SETS - 1, GROUPS - 1
        round_x(last - 1)
        round_page(last - 1)
        fetched[last] = keep.tile([P, NX], F32, name="fetched", tag=f"fetched{last % 2}")
        xmag_last = keep.tile([P, NX], F32, name="xmag", tag=f"mag{(last + 1) % 2}", align_bytes=64)
        nc.scalar.copy(out=page_bf[last_b][:, PACK - 1, 0 : T2 // 2], in_=pages[last][:, 0 : T2 // 2])
        for half in range(2):
            cols = slice(QUARTER * half, QUARTER * (half + 1))
            entries = ref[:, QUARTER // LIST_ROWS * half : QUARTER // LIST_ROWS * (half + 1)]
            nc.vector.tensor_copy(fetched[last][:, cols], pages[last][:].indirect(entries))
            round_x_columns(last, xmag_last, cols)

        def weave_page_quarter(k, copy):
            woven = keep.tile([P, QUARTER, PACK], BF16, name=f"quarter{k}", align_bytes=64)
            weave(copy, woven[:], page_bf[last_b], QUARTER * k, QUARTER * (k + 1))
            return woven

        def quantise_page_quarter(k, woven):
            cols = slice(QUARTER * (k % 2), QUARTER * (k % 2 + 1))
            quantise(woven, page_w[last_b][k // 2][:, cols], page_sc[last_b][k // 2][:, cols])

        first_quarter = weave_page_quarter(0, nc.vector.tensor_copy)
        x_woven = three.tile([P, PASS, PACK], BF16, name="woven", align_bytes=64)
        for c0, c1, copy in (
            (0, QUARTER, nc.vector.tensor_copy),
            (QUARTER, X_ON_VECTOR, nc.vector.tensor_copy),
            (X_ON_VECTOR, NX, nc.scalar.copy),
        ):
            weave(copy, x_woven[:, c0:c1, :], x_bf[last_b], c0, c1)
        quantise_page_quarter(0, first_quarter)
        quantise(x_woven, x_w[last_b][:], x_sc[last_b][:])
        nc.scalar.copy(out=page_bf[last_b][:, PACK - 1, T2 // 2 :], in_=pages[last][:, T2 // 2 :])

        for m in range(OUT_TILES):
            if m % 2 == 0 and m + 2 < OUT_TILES:
                quantise_page_quarter(m // 2 + 1, weave_page_quarter(m // 2 + 1, nc.scalar.copy))
            score_pass(banks[m], m, last_b)
            result = lims[m // PACK][:, m % PACK, :]
            nc.vector.tensor_tensor(out=result, in0=banks[m][:], in1=result, op=ALU.max)
            nc.sync.dma_start(out=out[P * m : P * (m + 1), :], in_=result)
